import numpy as np
import ml_dtypes


def mxq(x, axis, fmt="e4m3"):
    dtype, down = {"e4m3": (ml_dtypes.float8_e4m3fn, 7), "e5m2": (ml_dtypes.float8_e5m2, 14)}[fmt]
    v = np.moveaxis(np.asarray(x, np.float32).astype(ml_dtypes.bfloat16).astype(np.float64), axis, -1)
    blocks = v.reshape(v.shape[:-1] + (-1, 32))
    amax = np.abs(blocks).max(-1, keepdims=True)
    byte = np.maximum(np.where(amax > 0, np.frexp(amax)[1] - 1 + 127, 0) - down, 1)
    scale = np.exp2(byte - 127.0)
    codes = (blocks / scale).astype(np.float32).astype(dtype).astype(np.float64)
    return np.moveaxis((codes * scale).reshape(v.shape), -1, axis)


WIDE = False


def mx_kscale(k):
    if not WIDE:
        return np.ones(k)
    levels = np.array([10, -10, 5, -5, 0])
    if k % 512:
        return np.exp2(np.random.permutation(np.resize(levels, k // 32))).repeat(32)
    a = np.empty((k // 512, 16))
    for p in range(k // 512):
        a[p, :8] = np.random.permutation(np.resize(levels, 8))
        for g in range(8):
            far = levels[np.abs(levels - a[p, g]) >= 10]
            a[p, g + 8] = far[np.random.randint(len(far))]
    return np.exp2(a.ravel()).repeat(32)


def f64(x):
    return np.asarray(x).astype(np.float64)


def striped(idx):
    return np.tile(idx.reshape(-1, 16).T, (8, 1)).astype(np.uint16)


def unstriped(offs):
    return offs[:16].T.reshape(-1).astype(np.int64)


def pack_weight(w):
    k, n = w.shape
    w = f64(np.asarray(w, np.float32).astype(ml_dtypes.bfloat16)).reshape(k // 32, 32, n)
    amax = np.abs(w).max(1)
    byte = np.clip(np.where(amax > 0, np.frexp(amax)[1] - 1 + 127 - 7, 1), 1, 254)
    scaled = (w * np.exp2(127.0 - byte)[:, None, :]).reshape(k, n).astype(np.float32)
    words = np.ascontiguousarray(scaled.reshape(k // 512, 128, 4, n).transpose(0, 1, 3, 2)).astype(ml_dtypes.float8_e4m3fn).view(np.uint8)
    return words, np.ascontiguousarray(byte.astype(np.uint8).reshape(k // 512, 16, n))


def unpack_weight(words, scales):
    g, p, n, _ = words.shape
    vals = np.ascontiguousarray(words).view(ml_dtypes.float8_e4m3fn).astype(np.float64) * np.repeat(np.exp2(scales.astype(np.float64) - 127.0), 8, axis=1)[..., None]
    return vals.transpose(0, 1, 3, 2).reshape(g * 512, n)


K, T, S, N, V = 512, 2048, 512, 256, 256
P = 2 ** 7


def setup_inputs():
    n = np.random.standard_normal
    s = mx_kscale(K)[:, None]
    packed_xT = pack_weight(n((K, T)) * s)
    return {
        "x_words": packed_xT[0],
        "x_scales": packed_xT[1],
        "w1": (n((K, N)) / np.sqrt(K) / s).astype(np.float32),
        "rev": (np.tile(np.random.uniform(0.5, 3.0, V), (P, 1))).astype(np.float32),
        "offs": striped(np.random.permutation(T)[:S]),
        "cha": striped(np.random.randint(0, S, V)),
        "chb": striped(np.random.randint(0, S, V)),
        "chc": striped(np.random.randint(0, S, V)),
    }


def reference(x_words, x_scales, w1, rev, offs, cha, chb, chc):
    xq = unpack_weight(x_words, x_scales)[:, unstriped(offs)]
    y = mxq(f64(w1), 0, "e4m3").T @ xq
    stg = 0.7 * (np.log(np.exp(y) + 1.0))
    ea = stg[:, unstriped(cha)]
    wa = -1.0 * np.exp(-1.0 * ea) + 1.0
    eb = stg[:, unstriped(chb)]
    wab = -1.0 * (np.exp(-1.0 * (ea + eb))) + 1.0
    wb = -1.0 * np.exp(-1.0 * eb) + 1.0
    ec = stg[:, unstriped(chc)]
    wac = -1.0 * (np.exp(-1.0 * (ea + ec))) + 1.0
    wc = -1.0 * np.exp(-1.0 * ec) + 1.0
    wall = -1.0 * (np.exp(-1.0 * (ea + eb + ec))) + 1.0
    wbc = -1.0 * (np.exp(-1.0 * (eb + ec))) + 1.0
    return (wa / 3 + (wab - wb + wac - wc) / 6 + (wall - wbc) / 3) * f64(rev)[:1]

@@ -1,0 +1,125 @@
+from contextlib import ExitStack
+
+import concourse.mybir as mybir
+
+K, T, S, N, V = 512, 2048, 512, 256, 256
+P = 128
+PACK = 4
+HALF = S // 2
+FLOPS = 2 * K * S * N
+
+F32 = mybir.dt.float32
+BF16 = mybir.dt.bfloat16
+I32 = mybir.dt.int32
+U32 = mybir.dt.uint32
+U16 = mybir.dt.uint16
+U8 = mybir.dt.uint8
+FP8X4 = mybir.dt.float8_e4m3fn_x4
+ACT = mybir.ActivationFunctionType
+ALU = mybir.AluOpType
+
+LN_FLOOR = 2.0 ** -60
+
+
+def tile_picked_yshap_first_p_kernel(tc, x_words, x_scales, w1, rev, offs, cha, chb, chc, out):
+    nc = tc.nc
+    with ExitStack() as ctx:
+        keep = ctx.enter_context(tc.tile_pool(name="keep", bufs=1))
+        psum = ctx.enter_context(tc.psum_pool(name="psum", bufs=1))
+
+        offs_t = keep.tile([P, S // 16], U16, name="offs_t")
+        lists = [keep.tile([P, V // 16], U16, name="list%d" % i) for i in range(3)]
+        w_raw = keep.tile([P, PACK, N], F32, name="w_raw")
+        table_words = keep.tile([P, T], I32, name="table_words")
+        table_scales = keep.tile([P, T], U8, name="table_scales")
+        rev_t = keep.tile([P, V], F32, name="rev_t")
+
+        nc.vector.memset(table_scales[:].bitcast(I32), 0)
+        nc.sync.dma_start(offs_t[:], offs)
+        nc.sync.dma_start(w_raw[:], w1.rearrange("(p j) n -> p j n", j=PACK))
+        for q in range(4):
+            nc.sync.dma_start(
+                table_scales[32 * q : 32 * q + 4, :].bitcast(I32),
+                x_scales[0, 4 * q : 4 * q + 4, :].bitcast(I32),
+            )
+        nc.sync.dma_start(table_words[:], x_words[0].rearrange("p n t -> p (n t)").bitcast(I32))
+        for tile_, src in zip(lists, (cha, chb, chc)):
+            nc.sync.dma_start(tile_[:], src)
+        nc.sync.dma_start(rev_t[:], rev)
+
+        w_bf = keep.tile([P, N, PACK], BF16, name="w_bf", align_bytes=64)
+        nc.vector.tensor_copy(
+            out=w_bf[:].rearrange("p (c i) t -> p c t i", i=4),
+            in_=w_raw[:].rearrange("p t (c i) -> p c t i", i=4),
+        )
+        x_sc = keep.tile([P, S], U8, name="x_sc", align_bytes=64)
+        nc.vector.tensor_copy(x_sc[:], table_scales[:].indirect(offs_t[:]))
+        w_codes = keep.tile([P, N], U32, name="w_codes", align_bytes=64)
+        w_sc = keep.tile([P, N], U8, name="w_sc", align_bytes=64)
+        nc.vector.quantize_mx(
+            out=w_codes[:].bitcast(FP8X4), scales=w_sc[:], in_=w_bf[:].rearrange("p n t -> p (n t)")
+        )
+
+        sig = [keep.tile([P, S], F32, name="sig%d" % b) for b in range(2)]
+        for h in range(2):
+            x_codes = keep.tile([P, HALF], U32, name="x_codes%d" % h, align_bytes=64)
+            nc.vector.tensor_copy(
+                x_codes[:],
+                table_words[:].bitcast(U32).indirect(offs_t[:, h * HALF // 16 : (h + 1) * HALF // 16]),
+            )
+            cols = slice(h * HALF, (h + 1) * HALF)
+            for b in range(2):
+                y = psum.tile([P, HALF], F32, name="y%d%d" % (h, b))
+                rows = slice(b * P, (b + 1) * P)
+                nc.tensor.matmul_mx(
+                    out=y[:],
+                    lhsT=w_codes[:, rows].bitcast(FP8X4),
+                    lhsT_scale=w_sc[:, rows],
+                    rhs=x_codes[:].bitcast(FP8X4),
+                    rhs_scale=x_sc[:, cols],
+                    start=True,
+                    stop=True,
+                )
+                nc.scalar.activation(sig[b][:, cols], y[:], ACT.Sigmoid, scale=-1.0)
+
+        picked = keep.tile([P, 3, V], F32, name="picked")
+        for i in range(3):
+            nc.vector.tensor_copy(picked[:, i, :], sig[0][:].indirect(lists[i][:]))
+        log1 = keep.tile([P, S], F32, name="log1")
+        nc.scalar.activation(log1[:], sig[1][:], ACT.Ln, bias=LN_FLOOR)
+        logs = [keep.tile([P, 3, V], F32, name="logs%d" % b) for b in range(2)]
+        nc.scalar.activation(logs[0][:], picked[:], ACT.Ln, bias=LN_FLOOR)
+        for i in (2, 1, 0):
+            nc.vector.tensor_copy(logs[1][:, i, :], log1[:].indirect(lists[i][:]))
+
+        miss = [[keep.tile([P, V], F32, name="miss%d%d" % (b, i)) for i in range(3)] for b in range(2)]
+        for b in range(2):
+            for i in (2, 1, 0):
+                nc.scalar.activation(miss[b][i][:], logs[b][:, i, :], ACT.Exp, scale=0.7)
+
+        cn = [keep.tile([P, V], F32, name="cn%d" % b) for b in range(2)]
+        bc = [keep.tile([P, V], F32, name="bc%d" % b) for b in range(2)]
+        ar = [keep.tile([P, V], F32, name="ar%d" % b) for b in range(2)]
+        res = [keep.tile([P, V], F32, name="res%d" % b) for b in range(2)]
+
+        def shift_c(b):
+            nc.vector.tensor_scalar(cn[b][:], miss[b][2][:], -1.0 / 3.0, -1.0 / 6.0, ALU.mult, ALU.add)
+
+        def times_b(b):
+            nc.vector.scalar_tensor_tensor(bc[b][:], miss[b][1][:], 0.5, cn[b][:], ALU.add, ALU.mult)
+
+        def worth(b):
+            nc.vector.scalar_tensor_tensor(ar[b][:], miss[b][0][:], -1.0, rev_t[:], ALU.add, ALU.mult)
+
+        def finish(b):
+            nc.vector.scalar_tensor_tensor(res[b][:], bc[b][:], -0.25, ar[b][:], ALU.add, ALU.mult)
+            nc.sync.dma_start(out[b * P : (b + 1) * P, :], res[b][:])
+
+        shift_c(0)
+        times_b(0)
+        worth(0)
+        shift_c(1)
+        finish(0)
+        times_b(1)
+        worth(1)
+        finish(1)

@@ -35,8 +35,8 @@ def tile_picked_yshap_first_p_kernel(tc, x_words, x_scales, w1, rev, offs, cha, 
         rev_t = keep.tile([P, V], F32, name="rev_t")
 
         nc.vector.memset(table_scales[:].bitcast(I32), 0)
-        nc.sync.dma_start(offs_t[:], offs)
         nc.sync.dma_start(w_raw[:], w1.rearrange("(p j) n -> p j n", j=PACK))
+        nc.sync.dma_start(offs_t[:], offs)
         for q in range(4):
             nc.sync.dma_start(
                 table_scales[32 * q : 32 * q + 4, :].bitcast(I32),
@@ -67,20 +67,22 @@ def tile_picked_yshap_first_p_kernel(tc, x_words, x_scales, w1, rev, offs, cha, 
                 x_codes[:],
                 table_words[:].bitcast(U32).indirect(offs_t[:, h * HALF // 16 : (h + 1) * HALF // 16]),
             )
-            cols = slice(h * HALF, (h + 1) * HALF)
             for b in range(2):
-                y = psum.tile([P, HALF], F32, name="y%d%d" % (h, b))
                 rows = slice(b * P, (b + 1) * P)
-                nc.tensor.matmul_mx(
-                    out=y[:],
-                    lhsT=w_codes[:, rows].bitcast(FP8X4),
-                    lhsT_scale=w_sc[:, rows],
-                    rhs=x_codes[:].bitcast(FP8X4),
-                    rhs_scale=x_sc[:, cols],
-                    start=True,
-                    stop=True,
-                )
-                nc.scalar.activation(sig[b][:, cols], y[:], ACT.Sigmoid, scale=-1.0)
+                width = HALF // 2 if (h, b) == (1, 1) else HALF
+                for lo in range(0, HALF, width):
+                    cols = slice(h * HALF + lo, h * HALF + lo + width)
+                    y = psum.tile([P, width], F32, name="y%d%d%d" % (h, b, lo))
+                    nc.tensor.matmul_mx(
+                        out=y[:],
+                        lhsT=w_codes[:, rows].bitcast(FP8X4),
+                        lhsT_scale=w_sc[:, rows],
+                        rhs=x_codes[:, lo : lo + width].bitcast(FP8X4),
+                        rhs_scale=x_sc[:, cols],
+                        start=True,
+                        stop=True,
+                    )
+                    nc.scalar.activation(sig[b][:, cols], y[:], ACT.Sigmoid, scale=-1.0)
 
         picked = keep.tile([P, 3, V], F32, name="picked")
         for i in range(3):
@@ -93,8 +95,8 @@ def tile_picked_yshap_first_p_kernel(tc, x_words, x_scales, w1, rev, offs, cha, 
             nc.vector.tensor_copy(logs[1][:, i, :], log1[:].indirect(lists[i][:]))
 
         miss = [[keep.tile([P, V], F32, name="miss%d%d" % (b, i)) for i in range(3)] for b in range(2)]
-        for b in range(2):
-            for i in (2, 1, 0):
+        for i in (2, 1, 0):
+            for b in range(2):
                 nc.scalar.activation(miss[b][i][:], logs[b][:, i, :], ACT.Exp, scale=0.7)
 
         cn = [keep.tile([P, V], F32, name="cn%d" % b) for b in range(2)]
@@ -115,11 +117,6 @@ def tile_picked_yshap_first_p_kernel(tc, x_words, x_scales, w1, rev, offs, cha, 
             nc.vector.scalar_tensor_tensor(res[b][:], bc[b][:], -0.25, ar[b][:], ALU.add, ALU.mult)
             nc.sync.dma_start(out[b * P : (b + 1) * P, :], res[b][:])
 
-        shift_c(0)
-        times_b(0)
-        worth(0)
-        shift_c(1)
-        finish(0)
-        times_b(1)
-        worth(1)
-        finish(1)
+        for step in (shift_c, times_b, worth, finish):
+            for b in range(2):
+                step(b)

from contextlib import ExitStack

import concourse.mybir as mybir

K, T, S, N, V = 512, 2048, 512, 256, 256
P = 128
PACK = 4
HALF = S // 2
FLOPS = 2 * K * S * N

F32 = mybir.dt.float32
BF16 = mybir.dt.bfloat16
I32 = mybir.dt.int32
U32 = mybir.dt.uint32
U16 = mybir.dt.uint16
U8 = mybir.dt.uint8
FP8X4 = mybir.dt.float8_e4m3fn_x4
ACT = mybir.ActivationFunctionType
ALU = mybir.AluOpType

LN_FLOOR = 2.0 ** -60


def tile_picked_yshap_first_p_kernel(tc, x_words, x_scales, w1, rev, offs, cha, chb, chc, out):
    nc = tc.nc
    with ExitStack() as ctx:
        keep = ctx.enter_context(tc.tile_pool(name="keep", bufs=1))
        psum = ctx.enter_context(tc.psum_pool(name="psum", bufs=1))

        offs_t = keep.tile([P, S // 16], U16, name="offs_t")
        lists = [keep.tile([P, V // 16], U16, name="list%d" % i) for i in range(3)]
        w_raw = keep.tile([P, PACK, N], F32, name="w_raw")
        table_words = keep.tile([P, T], I32, name="table_words")
        table_scales = keep.tile([P, T], U8, name="table_scales")
        rev_t = keep.tile([P, V], F32, name="rev_t")

        nc.vector.memset(table_scales[:].bitcast(I32), 0)
        nc.sync.dma_start(w_raw[:], w1.rearrange("(p j) n -> p j n", j=PACK))
        nc.sync.dma_start(offs_t[:], offs)
        for q in range(4):
            nc.sync.dma_start(
                table_scales[32 * q : 32 * q + 4, :].bitcast(I32),
                x_scales[0, 4 * q : 4 * q + 4, :].bitcast(I32),
            )
        nc.sync.dma_start(table_words[:], x_words[0].rearrange("p n t -> p (n t)").bitcast(I32))
        for tile_, src in zip(lists, (cha, chb, chc)):
            nc.sync.dma_start(tile_[:], src)
        nc.sync.dma_start(rev_t[:], rev)

        w_bf = keep.tile([P, N, PACK], BF16, name="w_bf", align_bytes=64)
        nc.vector.tensor_copy(
            out=w_bf[:].rearrange("p (c i) t -> p c t i", i=4),
            in_=w_raw[:].rearrange("p t (c i) -> p c t i", i=4),
        )
        x_sc = keep.tile([P, S], U8, name="x_sc", align_bytes=64)
        nc.vector.tensor_copy(x_sc[:], table_scales[:].indirect(offs_t[:]))
        w_codes = keep.tile([P, N], U32, name="w_codes", align_bytes=64)
        w_sc = keep.tile([P, N], U8, name="w_sc", align_bytes=64)
        nc.vector.quantize_mx(
            out=w_codes[:].bitcast(FP8X4), scales=w_sc[:], in_=w_bf[:].rearrange("p n t -> p (n t)")
        )

        sig = [keep.tile([P, S], F32, name="sig%d" % b) for b in range(2)]
        for h in range(2):
            x_codes = keep.tile([P, HALF], U32, name="x_codes%d" % h, align_bytes=64)
            nc.vector.tensor_copy(
                x_codes[:],
                table_words[:].bitcast(U32).indirect(offs_t[:, h * HALF // 16 : (h + 1) * HALF // 16]),
            )
            for b in range(2):
                rows = slice(b * P, (b + 1) * P)
                width = HALF // 2 if (h, b) == (1, 1) else HALF
                for lo in range(0, HALF, width):
                    cols = slice(h * HALF + lo, h * HALF + lo + width)
                    y = psum.tile([P, width], F32, name="y%d%d%d" % (h, b, lo))
                    nc.tensor.matmul_mx(
                        out=y[:],
                        lhsT=w_codes[:, rows].bitcast(FP8X4),
                        lhsT_scale=w_sc[:, rows],
                        rhs=x_codes[:, lo : lo + width].bitcast(FP8X4),
                        rhs_scale=x_sc[:, cols],
                        start=True,
                        stop=True,
                    )
                    nc.scalar.activation(sig[b][:, cols], y[:], ACT.Sigmoid, scale=-1.0)

        picked = keep.tile([P, 3, V], F32, name="picked")
        for i in range(3):
            nc.vector.tensor_copy(picked[:, i, :], sig[0][:].indirect(lists[i][:]))
        log1 = keep.tile([P, S], F32, name="log1")
        nc.scalar.activation(log1[:], sig[1][:], ACT.Ln, bias=LN_FLOOR)
        logs = [keep.tile([P, 3, V], F32, name="logs%d" % b) for b in range(2)]
        nc.scalar.activation(logs[0][:], picked[:], ACT.Ln, bias=LN_FLOOR)
        for i in (2, 1, 0):
            nc.vector.tensor_copy(logs[1][:, i, :], log1[:].indirect(lists[i][:]))

        miss = [[keep.tile([P, V], F32, name="miss%d%d" % (b, i)) for i in range(3)] for b in range(2)]
        for i in (2, 1, 0):
            for b in range(2):
                nc.scalar.activation(miss[b][i][:], logs[b][:, i, :], ACT.Exp, scale=0.7)

        cn = [keep.tile([P, V], F32, name="cn%d" % b) for b in range(2)]
        bc = [keep.tile([P, V], F32, name="bc%d" % b) for b in range(2)]
        ar = [keep.tile([P, V], F32, name="ar%d" % b) for b in range(2)]
        res = [keep.tile([P, V], F32, name="res%d" % b) for b in range(2)]

        def shift_c(b):
            nc.vector.tensor_scalar(cn[b][:], miss[b][2][:], -1.0 / 3.0, -1.0 / 6.0, ALU.mult, ALU.add)

        def times_b(b):
            nc.vector.scalar_tensor_tensor(bc[b][:], miss[b][1][:], 0.5, cn[b][:], ALU.add, ALU.mult)

        def worth(b):
            nc.vector.scalar_tensor_tensor(ar[b][:], miss[b][0][:], -1.0, rev_t[:], ALU.add, ALU.mult)

        def finish(b):
            nc.vector.scalar_tensor_tensor(res[b][:], bc[b][:], -0.25, ar[b][:], ALU.add, ALU.mult)
            nc.sync.dma_start(out[b * P : (b + 1) * P, :], res[b][:])

        for step in (shift_c, times_b, worth, finish):
            for b in range(2):
                step(b)
